import numpy as np, ml_dtypes
CORES = [36,38,116,118,124,126,164,166,244,246,252,254]
N = 12
GR, GC, HH, WW = 4, 3, 8, 16
def setup_inputs(rng):
    return {"x": rng.standard_normal((N, 128, HH * WW), dtype=np.float32).astype(ml_dtypes.bfloat16), "w": rng.standard_normal((N, 128, 9 * 128), dtype=np.float32).astype(ml_dtypes.bfloat16)}
def setup_inputs_big(rng):
    d = setup_inputs(rng)
    for k in ("x", "w"): d[k] = (d[k].astype(np.float32) * 1024.0).astype(d[k].dtype)
    return d
def setup_inputs_small(rng):
    d = setup_inputs(rng)
    for k in ("x", "w"): d[k] = (d[k].astype(np.float32) * (1 / 1024.0)).astype(d[k].dtype)
    return d
def setup_inputs_apart(rng):
    d = setup_inputs(rng)
    f = (10.0 ** rng.permutation(np.linspace(-1.5, 1.5, N))).astype(np.float32).reshape(N, 1, 1)
    for k in ("x", "w"): d[k] = (d[k].astype(np.float32) * f).astype(d[k].dtype)
    return d
def reference(x, w):
    X = x.astype(np.float64).reshape(GR, GC, 128, HH, WW); W = w.astype(np.float64)
    g = np.concatenate([np.concatenate(list(X[i]), axis=2) for i in range(GR)], axis=1)
    y = np.zeros((N, 128, HH * WW))
    for r in range(N):
        i0, j0 = HH * (r // GC), WW * (r % GC)
        for a in range(3):
            for b in range(3):
                sh = np.roll(g, (-2 * (a - 1), -2 * (b - 1)), axis=(1, 2))[:, i0:i0 + HH, j0:j0 + WW]
                y[r] += W[r][:, 128 * (3 * a + b):128 * (3 * a + b) + 128].T @ sh.reshape(128, HH * WW)
    return {"y": y.astype(ml_dtypes.bfloat16 if x.dtype != np.float64 else np.float64)}

from concourse.bass import DstId, RemoteDMATransfer

GR, GC, HH, WW = 4, 3, 8, 16
HALO = 2
NENG = 8
SW = HALO * WW

SCRATCH = {
    "ds": ("dram", [2, 128, SW], "bfloat16"),
    "ld": ("dram", [2 * GC, 128, SW], "bfloat16"),
    "rl": ("dram", [2, 128, SW], "bfloat16"),
    "xs": ("sbuf", [128, HH, WW], "bfloat16"),
    "ws": ("sbuf", [128, 9 * 128], "bfloat16"),
    "pk": ("sbuf", [128, 4, HH, HALO], "bfloat16"),
    "hl": ("sbuf", [128, 2, HH, HALO], "bfloat16"),
    "hb": ("sbuf", [128, 2 * GC, HALO, WW], "bfloat16"),
    "ys": ("sbuf", [128, HH, WW], "bfloat16"),
    "ps": ("psum", [128, HH, WW], "float32"),
}
SEMAPHORES = (["dt", "db", "xl", "wl", "pv", "lh", "rh", "rq", "rl0", "rl1", "sent", "mm", "vc", "yd"]
              + ["ld%d" % k for k in range(2 * GC)] + ["hb%d" % k for k in range(2 * GC)])


def _sizes(n):
    base = 1
    while base * 2 * n <= NENG:
        base *= 2
    sizes, free = [base] * n, NENG - base * n
    for i in range(n):
        if free >= sizes[i]:
            free -= sizes[i]
            sizes[i] *= 2
    return sizes


def _plan(cores, topo):
    def rk(R, C):
        return cores[(R % GR) * GC + (C % GC)]

    def porter(q, dests):
        for c in cores:
            if (c != q and topo.host(c) == topo.host(q) and topo.chip(c) == topo.chip(q)
                    and all(topo.may_write(c, d) for d in dests)):
                return c
        raise ValueError("no rank on the chip of core %d can pass its data on" % q)

    own = {c: [] for c in cores}
    fwd = {c: [] for c in cores}
    fwd_wait = {c: [] for c in cores}
    late = {}
    for r, s in enumerate(cores):
        R, C = divmod(r, GC)
        feed, direct = [], []
        for side, dR, slot in ((0, -1, GC + C), (1, 1, C)):
            dests = [rk(R + dR, c) for c in range(GC)]
            ok = [d for d in dests if topo.may_write(s, d)]
            rest = [d for d in dests if d not in ok]
            sem = "ld%d" % slot
            for d in dests:
                late[(d, slot)] = d in rest
            if not rest:
                direct.append([("ds", side), [(d, ("ld", slot)) for d in ok], sem, 0])
                continue
            p = porter(s, rest)
            if p in ok:
                feed.append([("ds", side), [(d, ("ld", slot)) for d in [p] + [e for e in ok if e != p]], sem, 0])
                src, wait = ("ld", slot), sem
            else:
                feed.append([("ds", side), [(p, ("rl", side))], "rl%d" % side, 0])
                if ok:
                    direct.append([("ds", side), [(d, ("ld", slot)) for d in ok], sem, 0])
                src, wait = ("rl", side), "rl%d" % side
            fwd[p].append([src, [(d, ("ld", slot)) for d in rest], sem, 0])
            fwd_wait[p].append((wait, None))
        own[s] = feed + direct

    cols = {c: [] for c in cores}
    both = {c: [] for c in cores}
    joined = {}
    for r, s in enumerate(cores):
        R, C = divmod(r, GC)
        for slot, d, spare, span in ((1, rk(R, C - 1), 3, (2, 4)), (2, rk(R, C + 1), 0, (0, 2))):
            if topo.may_write(s, d):
                continue
            p = porter(s, [d])
            Rp, Cp = divmod(cores.index(p), GC)
            if rk(Rp, Cp + (1 if slot == 1 else -1)) != d:
                raise ValueError("the sibling has no pack for the same neighbour")
            cols[s].append([("pk", (slot, slot + 1)), [(p, ("pk", (spare, spare + 1)))], "rq", 0])
            both[p].append([("pk", span), [(d, ("hl", (0, 2)))], "lh", 0])
            joined[(s, slot)] = joined[(p, 3 - slot)] = True
    for r, s in enumerate(cores):
        R, C = divmod(r, GC)
        for slot, d, halo, sem in ((1, rk(R, C - 1), 1, "rh"), (2, rk(R, C + 1), 0, "lh")):
            if (s, slot) not in joined:
                cols[s].append([("pk", (slot, slot + 1)), [(d, ("hl", (halo, halo + 1)))], sem, 0])

    calls, inc, sent = {}, {}, {}
    for c in cores:
        calls[c] = [([("dt", 16), ("db", 16)], own[c])]
        if fwd[c]:
            calls[c].append((fwd_wait[c], fwd[c]))
        if cols[c]:
            calls[c].append(([("pv", 2)], cols[c]))
        if both[c]:
            calls[c].append(([("pv", 2), ("rq", None)], both[c]))
        sent[c] = 0
        for _, trs in calls[c]:
            for tr, size in zip(trs, _sizes(len(trs))):
                tr[3] = size
                sent[c] += size
                for d, _ in tr[1]:
                    inc[(d, tr[2])] = inc.get((d, tr[2]), 0) + size
    busy = {c: bool(fwd[c]) for c in cores}
    return calls, inc, sent, late, busy, both


def _work(C):
    own, lh, rh, st = [], [], [], {k: [] for k in range(2 * GC)}
    for a in (1, 0, 2):
        sr = HALO * (a - 1)
        ro = (max(0, -sr), min(HH, HH - sr))
        rs = (ro[0] + sr, ro[1] + sr)
        for b in (1, 0, 2):
            sc = HALO * (b - 1)
            co = (max(0, -sc), min(WW, WW - sc))
            cs = (co[0] + sc, co[1] + sc)
            tap = 3 * a + b
            left, right = (0, HALO), (WW - HALO, WW)
            own.append((tap, ro, co, rs, cs))
            if b == 0:
                lh.append((tap, ro, left, rs, (0, HALO)))
            if b == 2:
                rh.append((tap, ro, right, rs, (0, HALO)))
            if a != 1:
                base = 0 if a == 0 else GC
                rows = (0, HALO) if a == 0 else (HH - HALO, HH)
                st[base + C].append((tap, rows, co, (0, HALO), cs))
                if b == 0:
                    st[base + (C - 1) % GC].append((tap, rows, left, (0, HALO), right))
                if b == 2:
                    st[base + (C + 1) % GC].append((tap, rows, right, (0, HALO), left))
    return own, lh, rh, st


def rank_program(g, core, T, topo):
    rank = T.rank_of(core)
    if rank is None:
        return
    cores = list(T.cores)
    calls, inc, sent, late, busy, both = _plan(cores, topo)
    R, C = divmod(rank, GC)
    S = T.sem

    def place(p):
        name, i = p
        return T[name][:, i[0]:i[1]] if name in ("pk", "hl") else T[name][i]

    g.sync.dma_start(T.ds[0], T.x[:, 0:SW]).then_inc(S.dt, 16)
    g.scalar.dma_start(T.ds[1], T.x[:, HH * WW - SW:HH * WW]).then_inc(S.db, 16)
    g.sync.dma_start(T.xs[:], T.x[:, :]).then_inc(S.xl, 16)
    g.scalar.dma_start(T.ws[:], T.w[:, :]).then_inc(S.wl, 16)

    g.vector.wait_ge(S.xl, 16)
    g.vector.tensor_copy(T.pk[:, 1], T.xs[:, :, 0:HALO]).then_inc(S.pv, 1)
    g.vector.tensor_copy(T.pk[:, 2], T.xs[:, :, WW - HALO:WW]).then_inc(S.pv, 1)

    mask = -1
    for _, trs in calls[core]:
        for tr in trs:
            for d, _ in tr[1]:
                mask &= topo.mask(core, d)
    engines = [e for e in range(16) if (mask >> e) & 1][:NENG]
    for waits, trs in calls[core]:
        for name, n in waits:
            g.wait_ge(S[name], inc[(core, name)] if n is None else n)
        out, at = [], 0
        for src, dsts, sem, size in trs:
            m = sum(1 << e for e in engines[at:at + size])
            at += size
            ids = []
            for d, _ in dsts:
                rid, pid = topo.addr(d, core)
                ids.append(DstId(rid=rid, pnc=pid))
            out.append(RemoteDMATransfer(dst_ids=ids, dma_engine_mask=m, remote_sem=S[sem],
                                         srcs=[place(src)], dsts=[place(p) for _, p in dsts], alu_op=0))
        g.remote_dma_fused(out, local_sem=S.sent)
    g.wait_ge(S.sent, sent[core])

    for q, base in ((g.sync, 0), (g.scalar, GC)):
        for k in sorted(range(base, base + GC), key=lambda k: late[(core, k)]):
            q.wait_ge(S["ld%d" % k], inc[(core, "ld%d" % k)])
            q.dma_start(T.hb[:, k], T.ld[k]).then_inc(S["hb%d" % k], 16)

    own, lh, rh, st = _work(C)
    left_core = cores[R * GC + (C - 1) % GC]
    right_core = cores[R * GC + (C + 1) % GC]
    whole = (core, "rh") not in inc
    groups = [(0, [("xl", 16), ("wl", 16)], "xs", None, own)]
    groups.append((5 if whole else (3 if busy[left_core] else 1), [("lh", inc[(core, "lh")])], "hl", 0, lh))
    groups.append((5 if whole else (3 if busy[right_core] else 1),
                   [("lh", inc[(core, "lh")])] if whole else [("rh", inc[(core, "rh")])], "hl", 1, rh))
    for k in range(2 * GC):
        groups.append((6 if late[(core, k)] else 2, [("hb%d" % k, 16)], "hb", k, st[k]))
    groups.sort(key=lambda t: t[0])
    total = sum(len(t[4]) for t in groups)
    done = 0
    for _, waits, name, slot, mms in groups:
        for sem, n in waits:
            g.tensor.wait_ge(S[sem], n)
        for tap, ro, co, rs, cs in mms:
            src = T.xs[:, rs[0]:rs[1], cs[0]:cs[1]] if slot is None else T[name][:, slot, rs[0]:rs[1], cs[0]:cs[1]]
            done += 1
            mm = g.tensor.matmul(T.ps[:, ro[0]:ro[1], co[0]:co[1]], T.ws[:, 128 * tap:128 * tap + 128], src,
                                 done == 1, done == total)
            if done == total:
                mm.then_inc(S.mm, 1)

    g.vector.wait_ge(S.mm, 1)
    g.vector.tensor_copy(T.ys[:], T.ps[:]).then_inc(S.vc, 1)
    g.sync.wait_ge(S.vc, 1)
    g.sync.dma_start(T.y[:, :], T.ys[:]).then_inc(S.yd, 16)
    g.sync.wait_ge(S.yd, 16)
